import numpy as np
import ml_dtypes


def mxq(x, axis, fmt="e4m3"):
    dtype, down = {"e4m3": (ml_dtypes.float8_e4m3fn, 7), "e5m2": (ml_dtypes.float8_e5m2, 14)}[fmt]
    v = np.moveaxis(np.asarray(x, np.float32).astype(ml_dtypes.bfloat16).astype(np.float64), axis, -1)
    blocks = v.reshape(v.shape[:-1] + (-1, 32))
    amax = np.abs(blocks).max(-1, keepdims=True)
    byte = np.maximum(np.where(amax > 0, np.frexp(amax)[1] - 1 + 127, 0) - down, 1)
    scale = np.exp2(byte - 127.0)
    codes = (blocks / scale).astype(np.float32).astype(dtype).astype(np.float64)
    return np.moveaxis((codes * scale).reshape(v.shape), -1, axis)


WIDE = False


def mx_kscale(k):
    if not WIDE:
        return np.ones(k)
    levels = np.array([30, -30])
    if k % 512:
        return np.exp2(np.random.permutation(np.resize(levels, k // 32))).repeat(32)
    a = np.empty((k // 512, 16))
    for p in range(k // 512):
        a[p, :8] = np.random.permutation(np.resize(levels, 8))
        for g in range(8):
            far = levels[np.abs(levels - a[p, g]) >= 10]
            a[p, g + 8] = far[np.random.randint(len(far))]
    return np.exp2(a.ravel()).repeat(32)


def f64(x):
    return np.asarray(x).astype(np.float64)


def striped(idx):
    return np.tile(np.asarray(idx).reshape(-1, 16).T, (8, 1)).astype(np.uint16)


def unstriped(offs):
    return offs[:16].T.reshape(-1).astype(np.int64)


E2M1 = np.array([0.0, 0.5, 1.0, 1.5, 2.0, 3.0, 4.0, 6.0, -0.0, -0.5, -1.0, -1.5, -2.0, -3.0, -4.0, -6.0])


def pack_weight(w, fmt):
    k, n = w.shape
    w = f64(np.asarray(w, np.float32).astype(ml_dtypes.bfloat16)).reshape(k // 32, 32, n)
    amax = np.abs(w).max(1)
    if fmt in ("e4m3", "e5m2"):
        byte = np.frexp(amax)[1] - 1 + 127 - (7 if fmt == "e4m3" else 14)
    else:
        mant, ex = np.frexp(amax / 6.0)
        byte = np.where(mant > 0.5, ex, ex - 1) + 127
    byte = np.clip(np.where(amax > 0, byte, 1), 1, 254)
    scaled = (w * np.exp2(127.0 - byte)[:, None, :]).reshape(k, n).astype(np.float32)
    by_word = np.ascontiguousarray(scaled.reshape(k // 512, 128, 4, n).transpose(0, 1, 3, 2))
    if fmt in ("e4m3", "e5m2"):
        words = by_word.astype(ml_dtypes.float8_e4m3fn if fmt == "e4m3" else ml_dtypes.float8_e5m2).view(np.uint8)
    else:
        c = by_word.astype(ml_dtypes.float4_e2m1fn).view(np.uint8) & 0xF
        words = (c[..., 0::2] | (c[..., 1::2] << 4)).reshape(k // 512, 128, 2 * n)
    return np.ascontiguousarray(words), np.ascontiguousarray(byte.astype(np.uint8).reshape(k // 512, 16, n))


def unpack_weight(words, scales, fmt):
    g, _, n = scales.shape
    words = np.ascontiguousarray(words).reshape(g, 128, n, -1)
    if fmt in ("e4m3", "e5m2"):
        vals = words.view(ml_dtypes.float8_e4m3fn if fmt == "e4m3" else ml_dtypes.float8_e5m2).astype(np.float64)
    else:
        nib = np.empty((g, 128, n, 4), np.uint8)
        nib[..., 0::2] = words & 0xF
        nib[..., 1::2] = words >> 4
        vals = E2M1[nib]
    vals = vals * np.repeat(np.exp2(scales.astype(np.float64) - 127.0), 8, axis=1)[..., None]
    return vals.transpose(0, 1, 3, 2).reshape(g * 512, n)


K, T, J, R, F, Z, C, O, N, S = 512, 1024, 256, 512, 512, 1024, 512, 128, 256, 1024


def setup_inputs():
    n = np.random.standard_normal
    idx = np.random.permutation(T)[:J]
    idx2 = np.random.permutation(Z)[:J]
    idx3 = np.random.permutation(C)[:J]
    idx4 = np.random.permutation(C)[:O]
    idx5 = np.random.permutation(C)[:O]
    idx6 = np.random.permutation(J)[:O]
    idx7 = np.random.permutation(S)[:N]
    fk = mx_kscale(K)
    ff = mx_kscale(F)
    fr = mx_kscale(R)
    xtp = pack_weight(n((K, T)) / fk[:, None], "e2m1")
    xop = pack_weight(n((F, Z)) / ff[:, None], "e5m2")
    wp = pack_weight(n((K, R)) * 1 / np.sqrt(K) * fk[:, None] * fr, "e5m2")
    w0p = pack_weight(n((F, R)) * 1 / np.sqrt(F) * ff[:, None] * fr, "e4m3")
    w2p = pack_weight(n((F, R)) * 1 / np.sqrt(F) * ff[:, None], "e4m3")
    vsp = pack_weight(n((R, S)) * 1 / np.sqrt(R) / fr[:, None], "e4m3")
    return {
        "xt_words": xtp[0],
        "xt_scales": xtp[1],
        "xo_words": xop[0],
        "xo_scales": xop[1],
        "w_words": wp[0],
        "w_scales": wp[1],
        "w0_words": w0p[0],
        "w0_scales": w0p[1],
        "w2_words": w2p[0],
        "w2_scales": w2p[1],
        "vs_words": vsp[0],
        "vs_scales": vsp[1],
        "offs": striped(idx),
        "offs2": striped(idx2),
        "offs3": striped(idx3),
        "offs4": striped(idx4),
        "offs5": striped(idx5),
        "offs6": striped(idx6),
        "offs7": striped(idx7),
    }


def reference(xt_words, xt_scales, xo_words, xo_scales, w_words, w_scales, w0_words, w0_scales, w2_words, w2_scales, vs_words, vs_scales, offs, offs2, offs3, offs4, offs5, offs6, offs7):
    idx = unstriped(offs)
    idx2 = unstriped(offs2)
    idx3 = unstriped(offs3)
    idx4 = unstriped(offs4)
    idx5 = unstriped(offs5)
    idx6 = unstriped(offs6)
    idx7 = unstriped(offs7)
    xtu = unpack_weight(xt_words, xt_scales, "e2m1")
    xou = unpack_weight(xo_words, xo_scales, "e5m2")
    wu = unpack_weight(w_words, w_scales, "e5m2")
    w0u = unpack_weight(w0_words, w0_scales, "e4m3")
    w2u = unpack_weight(w2_words, w2_scales, "e4m3")
    vsu = unpack_weight(vs_words, vs_scales, "e4m3")
    xtidxg = xtu[:, idx]
    xoidx2g = xou[:, idx2]
    a = wu.T @ xtidxg + w0u.T @ xoidx2g
    b = w2u.T @ xoidx2g
    lb = b[:, 0:1]
    lb2 = b[:, 128:129]
    la = a[:, 0:1]
    pw = np.zeros((R, C))
    pw[:, idx3] = a
    hid = np.maximum(pw[:, idx4] * lb, pw[:, idx5] * lb2) - b[:, idx6] * la
    vsidx7g = vsu[:, idx7]
    hidq = mxq(hid, 0, "e5m2")
    y = vsidx7g.T @ hidq
    return y

from contextlib import ExitStack

import concourse.mybir as mybir

FLOPS = 436207616
F32 = mybir.dt.float32
BF16 = mybir.dt.bfloat16
I32 = mybir.dt.int32
U32 = mybir.dt.uint32
U16 = mybir.dt.uint16
U8 = mybir.dt.uint8
E4M3 = mybir.dt.float8_e4m3fn_x4
E5M2 = mybir.dt.float8_e5m2_x4
E2M1 = mybir.dt.float4_e2m1fn_x4
COPY = mybir.ActivationFunctionType.Copy
ALU = mybir.AluOpType
P = 128
DIRECT = ("xt", "vs",)
T, J, R, C, O = 1024, 256, 512, 512, 128


def tile_list_leadreads_noted_store_plain_kernel(
    tc, xt_words, xt_scales, xo_words, xo_scales, w_words, w_scales, w0_words, w0_scales,
    w2_words, w2_scales, vs_words, vs_scales, offs, offs2, offs3, offs4, offs5, offs6, offs7, out,
):
    nc = tc.nc
    with ExitStack() as ctx:
        lists = ctx.enter_context(tc.tile_pool(name="lists", bufs=1))
        sb = ctx.enter_context(tc.tile_pool(name="sb", bufs=1))
        ps = ctx.enter_context(tc.psum_pool(name="ps", bufs=1))

        def tile(name, shape, dtype):
            return sb.tile(shape, dtype, name=name, align_bytes=64)

        lst = {}
        for name, ap in (("l1", offs), ("l2", offs2), ("l3", offs3), ("l4", offs4), ("l5", offs5), ("l6", offs6), ("l7", offs7)):
            lst[name] = (lists.tile(list(ap.shape), U16, name=name), ap)

        def load_list(name):
            nc.sync.dma_start(lst[name][0][:], lst[name][1])

        def L(name):
            return lst[name][0][:]

        cols = {"xo": T, "xt": T, "vs": T, "w2": R, "w0": R, "w": R}
        scales_in = {"xo": xo_scales, "xt": xt_scales, "vs": vs_scales, "w2": w2_scales, "w0": w0_scales, "w": w_scales}
        WEIGHTS = ("w2", "w0", "w")
        plane = {k: tile("plane_" + k, [P, T], U8) for k in ("xo", "xt", "vs")}
        stage = {k: tile("stage_" + k, [4, 4, T // 4], I32) for k in plane if k not in DIRECT}
        w_stage = tile("w_stage", [4, 4, 3, R // 4], I32)
        w_plane = tile("w_plane", [P, 3, R // 4], I32)
        w_dealt = tile("w_dealt", [P, 3, R], U8)

        def clear_plane(k):
            nc.vector.memset(plane[k][:].bitcast(I32), 0)

        def load_scales(k, eng):
            rows = scales_in[k][0].bitcast(I32)
            if k in DIRECT:
                for q in range(4):
                    src = rows[4 * q : 4 * q + 4].unsqueeze(0).broadcast_to([8, 4, cols[k] // 4])
                    eng.dma_start(plane[k][32 * q : 32 * q + 32].bitcast(I32), src)
            else:
                dst = w_stage[:, :, WEIGHTS.index(k), :] if k in WEIGHTS else stage[k][:]
                eng.dma_start(dst, rows.rearrange("(q r) n -> r q n", q=4))

        def spread(k):
            for q in range(4):
                nc.vector.tensor_copy(plane[k][32 * q : 32 * q + 4].bitcast(I32), stage[k][:, q, :])

        words_in = {"xo": xo_words, "vs": vs_words, "w2": w2_words, "w0": w0_words, "w": w_words}
        words = {k: tile("words_" + k, [P, cols[k]], U32) for k in words_in}
        words["xt"] = tile("words_xt", [P, T], U16)

        def load_words(k, eng):
            if k == "xt":
                src = xt_words[0].bitcast(I32)
            else:
                src = words_in[k][0].rearrange("p n t -> p (n t)").bitcast(I32)
            eng.dma_start(words[k][:].bitcast(I32), src)

        gw = {"xo": tile("gw_xo", [P, J], U32), "xt": tile("gw_xt", [P, J], U16), "vs": tile("gw_vs", [P, J], U32)}
        gs = {k: tile("gs_" + k, [P, J], U8) for k in ("xo", "xt", "vs")}
        which = {"xo": "l2", "xt": "l1", "vs": "l7"}

        def gather_words(k):
            nc.vector.tensor_copy(gw[k][:], words[k][:].indirect(L(which[k])))

        def gather_scales(k):
            nc.vector.tensor_copy(gs[k][:], plane[k][:].indirect(L(which[k])))

        dealt_w = {k: tile("dealt_w_" + k, [P, R], U32) for k in ("w2", "w0", "w")}
        dealt_s = {k: w_dealt[:, i, :] for i, k in enumerate(WEIGHTS)}

        def spread_w():
            for q in range(4):
                nc.vector.tensor_copy(w_plane[32 * q : 32 * q + 4], w_stage[:, q])

        def deal_scales(eng, i0, i1):
            eng.tensor_copy(
                w_dealt[:, i0:i1, :].rearrange("p k (t m) -> p t k m", t=4),
                w_plane[:, i0:i1, :].bitcast(U8).rearrange("p k (m t) -> p t k m", t=4),
            )

        def deal_words(k):
            nc.scalar.copy(
                dealt_w[k][:].rearrange("p (t c i) -> p c t i", t=4, i=4),
                words[k][:].rearrange("p (c i t) -> p c t i", t=4, i=4),
            )

        board = [tile("board%d" % t, [P, C], F32) for t in range(4)]
        a_sb = [tile("a%d" % t, [P, J], F32) for t in range(4)]
        b_sb = [tile("b%d" % t, [P, J], F32) for t in range(4)]
        a_ps = [ps.tile([P, J], F32, name="a_ps%d" % t) for t in range(4)]
        b_ps = [ps.tile([P, J], F32, name="b_ps%d" % t) for t in range(4)]
        xs = [tile("x%d" % u, [P, 2, O], F32) for u in range(2)]
        ys = [tile("y%d" % u, [P, 2, O], F32) for u in range(2)]
        zs = [tile("z%d" % u, [P, 2, O], F32) for u in range(2)]
        ms = [tile("m%d" % u, [P, 2, O], F32) for u in range(2)]
        hid = tile("hid", [P, O, 4], BF16)
        hid_w = tile("hid_w", [P, O], U32)
        hid_s = tile("hid_s", [P, O], U8)

        def mm_b(t):
            c = slice(P * t, P * t + P)
            nc.tensor.matmul_mx(b_ps[t][:], lhsT=dealt_w["w2"][:, c].bitcast(E4M3), lhsT_scale=dealt_s["w2"][:, c],
                                rhs=gw["xo"][:].bitcast(E5M2), rhs_scale=gs["xo"][:], start=True, stop=True)

        def mm_a(t):
            c = slice(P * t, P * t + P)
            nc.tensor.matmul_mx(a_ps[t][:], lhsT=dealt_w["w0"][:, c].bitcast(E4M3), lhsT_scale=dealt_s["w0"][:, c],
                                rhs=gw["xo"][:].bitcast(E5M2), rhs_scale=gs["xo"][:], start=True, stop=False)
            nc.tensor.matmul_mx(a_ps[t][:], lhsT=dealt_w["w"][:, c].bitcast(E5M2), lhsT_scale=dealt_s["w"][:, c],
                                rhs=gw["xt"][:].bitcast(E2M1), rhs_scale=gs["xt"][:], start=False, stop=True)

        def evac(eng, dst, src):
            if eng == "v":
                nc.vector.tensor_copy(dst, src)
            else:
                nc.scalar.copy(dst, src)

        def scatter(eng, t):
            if eng == "v":
                nc.vector.tensor_copy(board[t][:].indirect(L("l3")), a_sb[t][:])
            else:
                nc.scalar.activation(out=board[t][:].indirect(L("l3")), in_=a_sb[t][:], func=COPY)

        def fetch_z(t):
            nc.scalar.activation(out=zs[t // 2][:, t % 2, :], in_=b_sb[t][:].indirect(L("l6")), func=COPY, scale=a_sb[t][:, 0:1])

        def fetch_xy(t):
            nc.scalar.activation(out=xs[t // 2][:, t % 2, :], in_=board[t][:].indirect(L("l4")), func=COPY, scale=b_sb[t][:, 0:1])
            nc.scalar.activation(out=ys[t // 2][:, t % 2, :], in_=board[t][:].indirect(L("l5")), func=COPY, scale=b_sb[t][:, 128:129])

        def larger(t):
            nc.vector.tensor_tensor(ms[t // 2][:, t % 2, :], xs[t // 2][:, t % 2, :], ys[t // 2][:, t % 2, :], ALU.max)

        def finish(u):
            nc.vector.tensor_tensor(hid[:, :, 2 * u : 2 * u + 2], ms[u][:].rearrange("p t o -> p o t"),
                                    zs[u][:].rearrange("p t o -> p o t"), ALU.subtract)

        clear_plane("xo")
        nc.vector.memset(w_plane[:], 0)
        for t in range(4):
            nc.gpsimd.memset(board[t][:], 0.0)
        load_scales("xo", nc.sync)
        load_scales("w2", nc.sync)
        load_scales("w0", nc.sync)
        load_scales("w", nc.sync)
        load_list("l2")
        load_list("l1")
        load_words("xo", nc.sync)
        load_words("w2", nc.sync)
        load_words("w0", nc.sync)
        load_words("w", nc.sync)
        load_scales("xt", nc.sync)
        load_words("xt", nc.sync)
        load_list("l3")
        load_words("vs", nc.sync)
        load_list("l7")
        load_scales("vs", nc.sync)
        for n in ("l6", "l4", "l5"):
            load_list(n)
        spread("xo")
        spread_w()
        gather_scales("xo")
        gather_words("xo")
        deal_scales(nc.vector, 0, 3)
        deal_words("w2")
        deal_words("w0")
        deal_words("w")
        for t in (0, 3, 1, 2):
            mm_b(t)
        gather_scales("xt")
        gather_words("xt")
        for t in (0, 3, 1, 2):
            evac("s", b_sb[t][:], b_ps[t][:])
        for t in (0, 3, 1, 2):
            mm_a(t)
        gather_scales("vs")
        evac("v", a_sb[0][:], a_ps[0][:])
        scatter("v", 0)
        evac("s", a_sb[3][:], a_ps[3][:])
        evac("s", a_sb[1][:], a_ps[1][:])
        scatter("s", 3)
        scatter("v", 1)
        evac("s", a_sb[2][:], a_ps[2][:])
        scatter("v", 2)
        for t in (0, 3, 1):
            fetch_xy(t)
            fetch_z(t)
        gather_words("vs")
        larger(0)
        larger(1)
        finish(0)
        larger(3)
        fetch_xy(2)
        fetch_z(2)
        larger(2)
        finish(1)

        nc.vector.quantize_mx(out=hid_w[:].bitcast(E5M2), scales=hid_s[:], in_=hid[:].rearrange("p o t -> p (o t)"))
        for h in range(2):
            c = slice(P * h, P * h + P)
            y_ps = ps.tile([P, O], F32, name="y_ps%d" % h, tag="b_ps%d" % h)
            nc.tensor.matmul_mx(y_ps[:], lhsT=gw["vs"][:, c].bitcast(E4M3), lhsT_scale=gs["vs"][:, c],
                                rhs=hid_w[:].bitcast(E5M2), rhs_scale=hid_s[:], start=True, stop=True)
            y_sb = tile("y_sb%d" % h, [P, O], F32)
            evac("sv"[h], y_sb[:], y_ps[:])
            (nc.scalar, nc.sync)[h].dma_start(out[c, :], y_sb[:])
